import numpy as np
import ml_dtypes


def mxq(x, axis, fmt="e4m3"):
    dtype, down = {"e4m3": (ml_dtypes.float8_e4m3fn, 7), "e5m2": (ml_dtypes.float8_e5m2, 14)}[fmt]
    v = np.moveaxis(np.asarray(x, np.float32).astype(ml_dtypes.bfloat16).astype(np.float64), axis, -1)
    blocks = v.reshape(v.shape[:-1] + (-1, 32))
    amax = np.abs(blocks).max(-1, keepdims=True)
    byte = np.maximum(np.where(amax > 0, np.frexp(amax)[1] - 1 + 127, 0) - down, 1)
    scale = np.exp2(byte - 127.0)
    codes = (blocks / scale).astype(np.float32).astype(dtype).astype(np.float64)
    return np.moveaxis((codes * scale).reshape(v.shape), -1, axis)


WIDE = False


def mx_kscale(k):
    if not WIDE:
        return np.ones(k)
    levels = np.array([30, -30])
    if k % 512:
        return np.exp2(np.random.permutation(np.resize(levels, k // 32))).repeat(32)
    a = np.empty((k // 512, 16))
    for p in range(k // 512):
        a[p, :8] = np.random.permutation(np.resize(levels, 8))
        for g in range(8):
            far = levels[np.abs(levels - a[p, g]) >= 10]
            a[p, g + 8] = far[np.random.randint(len(far))]
    return np.exp2(a.ravel()).repeat(32)


BF16 = ml_dtypes.bfloat16


def bf(x):
    return np.asarray(x, np.float32).astype(BF16)


def f64(x):
    return np.asarray(x).astype(np.float64)


M, T, L = 1024, 1024, 1536


def setup_inputs():
    s = mx_kscale(T)
    t = mx_kscale(L)
    thrust = np.exp(0.6 * np.random.standard_normal((M, T)))
    area = np.random.uniform(0.5, 2.0, T)
    kern = np.square(np.random.standard_normal((T, T))) / (20.0 * T)
    outer = np.random.exponential(1.0, (M, L))
    okern = np.random.standard_normal((L, T)) ** 4 / (24.0 * L)
    inflow = np.random.uniform(1.3, 1.7, M)
    return {"thrust": bf(thrust),
            "area": bf(area * s),
            "kern": bf(kern / s[:, None]),
            "outer": bf(outer * t),
            "okern": bf(okern / t[:, None]),
            "inflow": bf(inflow)}


def reference(thrust, area, kern, outer, okern, inflow):
    a = np.square(f64(thrust)) * f64(area)
    own = mxq(a, 1, "e5m2") @ mxq(f64(kern), 0, "e4m3")
    ext = mxq(f64(outer), 1, "e4m3") @ mxq(f64(okern), 0, "e4m3")
    d2 = own + ext
    speed = f64(inflow)[:, None] - np.sqrt(d2)
    power = speed ** 3
    return speed, power

@@ -1,0 +1,333 @@
+from contextlib import ExitStack
+
+import concourse.mybir as mybir
+from concourse.masks import make_identity
+
+M, T, L, N = 1024, 1024, 1536, 1024
+FLOPS = 2 * M * N * (T + L)
+
+F32 = mybir.dt.float32
+BF16 = mybir.dt.bfloat16
+U32 = mybir.dt.uint32
+U8 = mybir.dt.uint8
+E4M3 = mybir.dt.float8_e4m3fn_x4
+E5M2 = mybir.dt.float8_e5m2_x4
+ACT = mybir.ActivationFunctionType
+ALU = mybir.AluOpType
+
+P = 128
+KP = 512
+GT = T // KP
+GL = L // KP
+NW = GT + GL
+ROWS = M // P
+PAIRS = ROWS // 2
+H = 512
+
+
+def tile_wind_farm_wakes_s2_kernel(tc, thrust, area, kern, outer, okern, inflow, speed, power):
+    nc = tc.nc
+    with ExitStack() as ctx:
+        keep = ctx.enter_context(tc.tile_pool(name="keep", bufs=1))
+        work = ctx.enter_context(tc.tile_pool(name="work", bufs=2))
+        turn = ctx.enter_context(tc.psum_pool(name="turn", bufs=4))
+        sums = ctx.enter_context(tc.psum_pool(name="sums", bufs=4))
+        ctx.enter_context(tc.manual_schedule())
+
+        ident = keep.tile([P, P], F32, name="ident")
+        make_identity(nc, ident[:])
+        dummy = keep.tile([P, 1], F32, name="dummy")
+        nc.gpsimd.memset(dummy[:], 1.0)
+        nc.scalar.activation(out=dummy[:], in_=dummy[:], func=ACT.Sqrt)
+        area_b = keep.tile([P, GT, 4], BF16, name="area_b")
+        inflow_b = keep.tile([P, ROWS], BF16, name="inflow_b")
+        nc.scalar.dma_start(out=area_b[:], in_=area.rearrange("(g p j) -> p g j", g=GT, j=4))
+        nc.scalar.dma_start(out=inflow_b[:], in_=inflow.rearrange("(p t) -> p t", t=ROWS))
+        inflow_f = keep.tile([P, ROWS], F32, name="inflow_f")
+
+        w_hbm = [kern[g * KP:(g + 1) * KP, :] for g in range(GT)] + [okern[g * KP:(g + 1) * KP, :] for g in range(GL)]
+        w_raw = {}
+        t_raw = {}
+        o_raw = {}
+
+        def load_w(w, c0, width):
+            raw = keep.tile([P, 4, width], BF16, name="w_raw_%d_%d" % (w, c0), align_bytes=64)
+            nc.sync.dma_start(out=raw[:], in_=w_hbm[w].rearrange("(p j) n -> p j n", j=4)[:, :, c0:c0 + width])
+            for h in range(2):
+                if c0 <= h * H < c0 + width:
+                    w_raw[w, h] = raw[:, :, h * H - c0:h * H - c0 + H]
+
+        def load_x(i):
+            t_raw[i] = keep.tile([P, 2, T], BF16, name="t_raw_%d" % i, align_bytes=64)
+            nc.sync.dma_start(out=t_raw[i][:], in_=thrust.rearrange("(p t) k -> p t k", t=ROWS)[:, 2 * i:2 * i + 2, :])
+            o_raw[i] = keep.tile([P, 2, L], BF16, name="o_raw_%d" % i, align_bytes=64)
+            nc.sync.dma_start(out=o_raw[i][:], in_=outer.rearrange("(p t) k -> p t k", t=ROWS)[:, 2 * i:2 * i + 2, :])
+
+        load_w(0, 0, H)
+        load_w(0, H, H)
+        load_x(0)
+        load_w(1, 0, N)
+        load_w(2, 0, N)
+        load_x(1)
+        load_w(3, 0, N)
+        load_w(4, 0, N)
+        load_x(2)
+        load_x(3)
+
+        w_codes = [keep.tile([P, N], U32, name="w_codes_%d" % w, align_bytes=64) for w in range(NW)]
+        w_scales = [keep.tile([P, N], U8, name="w_scales_%d" % w, align_bytes=64) for w in range(NW)]
+        w_lay = {}
+
+        def lay(w, h, copy):
+            dst = work.tile([P, H, 4], BF16, name="w_lay", bufs=3, align_bytes=64)
+            w_lay[w, h] = dst
+            copy(
+                out=dst[:].rearrange("p (c i) j -> p c j i", i=4),
+                in_=w_raw[w, h].rearrange("p j (c i) -> p c j i", i=4),
+            )
+
+        def quant_w(w, h):
+            cols = slice(h * H, (h + 1) * H)
+            nc.vector.quantize_mx(
+                out=w_codes[w][:, cols].bitcast(E4M3),
+                scales=w_scales[w][:, cols],
+                in_=w_lay[w, h][:].rearrange("p c j -> p (c j)"),
+            )
+
+        x_codes = {}
+        x_scales = {}
+        for i in range(PAIRS):
+            x_codes[i] = keep.tile([P, NW, 2 * P], U32, name="x_codes_%d" % i, align_bytes=64)
+            x_scales[i] = keep.tile([P, NW, 2 * P], U8, name="x_scales_%d" % i, align_bytes=64)
+
+        banks = {}
+
+        def turn_x(raw, g):
+            bank = turn.tile([P, 2, 2 * P], F32, name="bank")
+            words = raw[:].bitcast(F32)
+            for mt in range(2):
+                for u in range(2):
+                    nc.tensor.transpose(
+                        bank[:, u, mt * P:(mt + 1) * P],
+                        words[:, mt, 256 * g + u:256 * (g + 1):2],
+                        ident[:],
+                    )
+            return bank
+
+        t_sq = {}
+        t_a = {}
+        o_lay = {}
+
+        def turn_t(i):
+            for g in range(GT):
+                banks["t", i, g] = turn_x(t_raw[i], g)
+
+        def turn_o(i):
+            for g in range(GL):
+                banks["o", i, g] = turn_x(o_raw[i], g)
+
+        def square_t(i, g):
+            if g == 0:
+                t_sq[i] = work.tile([P, GT, 2 * P, 4], F32, name="t_sq", bufs=2, align_bytes=64)
+            nc.scalar.activation(
+                out=t_sq[i][:, g].rearrange("p c (u e) -> p c u e", e=2),
+                in_=banks["t", i, g][:].bitcast(BF16).rearrange("p u (c e) -> p c u e", e=2),
+                func=ACT.Square,
+            )
+
+        def area_t(i, g):
+            if g == 0:
+                t_a[i] = work.tile([P, GT, 2 * P, 4], BF16, name="t_a", bufs=2, align_bytes=64)
+            nc.vector.tensor_tensor(
+                out=t_a[i][:, g],
+                in0=t_sq[i][:, g],
+                in1=area_b[:, g, :].unsqueeze(1).to_broadcast([P, 2 * P, 4]),
+                op=ALU.mult,
+            )
+
+        def quant_t(i):
+            nc.vector.quantize_mx(
+                out=x_codes[i][:, 0:GT, :].rearrange("p g c -> p (g c)").bitcast(E5M2),
+                scales=x_scales[i][:, 0:GT, :].rearrange("p g c -> p (g c)"),
+                in_=t_a[i][:].rearrange("p g c j -> p (g c j)"),
+            )
+
+        def lay_o(i, g):
+            if g == 0:
+                o_lay[i] = work.tile([P, GL, 2 * P, 2], F32, name="o_lay", bufs=2, align_bytes=64)
+            nc.scalar.copy(out=o_lay[i][:, g], in_=banks["o", i, g][:].rearrange("p u c -> p c u"))
+
+        def quant_o(i):
+            src = o_lay[i][:].rearrange("p g c u -> p g (c u)").bitcast(BF16)
+            for g0, g1 in ((0, 2), (2, 3)):
+                nc.vector.quantize_mx(
+                    out=x_codes[i][:, GT + g0:GT + g1, :].rearrange("p g c -> p (g c)").bitcast(E4M3),
+                    scales=x_scales[i][:, GT + g0:GT + g1, :].rearrange("p g c -> p (g c)"),
+                    in_=src[:, g0:g1, :].rearrange("p g c -> p (g c)"),
+                )
+
+        acc = {}
+
+        def mx(i, mt, h, passes):
+            if 0 in passes:
+                acc[i, mt, h] = sums.tile([P, H], F32, name="acc")
+            rows = slice(mt * P, (mt + 1) * P)
+            cols = slice(h * H, (h + 1) * H)
+            for w in passes:
+                nc.tensor.matmul_mx(
+                    out=acc[i, mt, h][:],
+                    lhsT=x_codes[i][:, w, rows].bitcast(E5M2 if w < GT else E4M3),
+                    lhsT_scale=x_scales[i][:, w, rows],
+                    rhs=w_codes[w][:, cols].bitcast(E4M3),
+                    rhs_scale=w_scales[w][:, cols],
+                    start=(w == 0),
+                    stop=(w == NW - 1),
+                )
+
+        def mx_all(i, passes):
+            for mt in range(2):
+                for h in range(2):
+                    mx(i, mt, h, passes)
+
+        root = {}
+        vel = {}
+        vel2 = {}
+        pw = {}
+
+        def root_d2(i, mt, h):
+            if h == 0:
+                root[i, mt] = work.tile([P, N], F32, name="root", bufs=2)
+            nc.scalar.activation(out=root[i, mt][:, h * H:(h + 1) * H], in_=acc[i, mt, h][:], func=ACT.Sqrt)
+
+        def square_v(i, mt, c0=0, c1=N):
+            r = 2 * i + mt
+            if c0 == 0:
+                vel2[i, mt] = work.tile([P, N], F32, name="vel2", bufs=2)
+            nc.scalar.activation(
+                out=vel2[i, mt][:, c0:c1], in_=root[i, mt][:, c0:c1], func=ACT.Square, scale=-1.0, bias=inflow_f[:, r:r + 1]
+            )
+
+        def speed_v(i, mt, c0=0, c1=N):
+            r = 2 * i + mt
+            if c0 == 0:
+                vel[i, mt] = work.tile([P, N], F32, name="vel", bufs=3)
+            nc.vector.tensor_scalar(
+                out=vel[i, mt][:, c0:c1], in0=root[i, mt][:, c0:c1], scalar1=-1.0, scalar2=inflow_f[:, r:r + 1],
+                op0=ALU.mult, op1=ALU.add,
+            )
+            nc.sync.dma_start(out=speed.rearrange("(p t) n -> p t n", t=ROWS)[:, r, c0:c1], in_=vel[i, mt][:, c0:c1])
+
+        def power_v(i, mt, c0=0, c1=N):
+            r = 2 * i + mt
+            if c0 == 0:
+                pw[i, mt] = work.tile([P, N], F32, name="pw", bufs=3)
+            nc.vector.tensor_tensor(
+                out=pw[i, mt][:, c0:c1], in0=vel2[i, mt][:, c0:c1], in1=vel[i, mt][:, c0:c1], op=ALU.mult
+            )
+            nc.sync.dma_start(out=power.rearrange("(p t) n -> p t n", t=ROWS)[:, r, c0:c1], in_=pw[i, mt][:, c0:c1])
+
+        act_copy = nc.scalar.copy
+        dve_copy = nc.vector.tensor_copy
+
+        lay(0, 0, act_copy)
+        nc.vector.tensor_copy(out=inflow_f[:], in_=inflow_b[:])
+        lay(0, 1, dve_copy)
+        turn_t(0)
+        square_t(0, 0)
+        quant_w(0, 0)
+        quant_w(0, 1)
+        square_t(0, 1)
+        area_t(0, 0)
+        turn_o(0)
+        lay_o(0, 0)
+        lay_o(0, 1)
+        lay_o(0, 2)
+        area_t(0, 1)
+        lay(1, 1, dve_copy)
+        lay(1, 0, act_copy)
+        quant_t(0)
+        quant_o(0)
+        lay(2, 1, dve_copy)
+        quant_w(1, 1)
+        quant_w(1, 0)
+        mx_all(0, [0])
+        lay(2, 0, act_copy)
+        quant_w(2, 1)
+        turn_t(1)
+        mx_all(0, [1])
+        square_t(1, 0)
+        square_t(1, 1)
+        quant_w(2, 0)
+        area_t(1, 0)
+        turn_o(1)
+        lay_o(1, 0)
+        lay_o(1, 1)
+        lay_o(1, 2)
+        lay(3, 1, dve_copy)
+        area_t(1, 1)
+        mx_all(0, [2])
+        lay(3, 0, act_copy)
+        quant_w(3, 1)
+        quant_t(1)
+        lay(4, 0, dve_copy)
+        quant_o(1)
+        quant_w(3, 0)
+        lay(4, 1, dve_copy)
+        quant_w(4, 0)
+        turn_t(2)
+        square_t(2, 0)
+        square_t(2, 1)
+        turn_o(2)
+        lay_o(2, 0)
+        lay_o(2, 1)
+        lay_o(2, 2)
+        area_t(2, 0)
+        quant_w(4, 1)
+        mx_all(0, [3, 4])
+
+        for i in range(PAIRS):
+            n = i + 3
+            m = i + 2
+            ahead = n < PAIRS
+            feed = m < PAIRS
+            last = i == PAIRS - 1
+            root_d2(i, 0, 0)
+            root_d2(i, 0, 1)
+            if ahead:
+                turn_t(n)
+            if feed and i > 0:
+                area_t(m, 0)
+            if not last:
+                mx(i + 1, 0, 0, range(NW))
+                mx(i + 1, 0, 1, range(NW))
+            square_v(i, 0)
+            speed_v(i, 0)
+            if ahead:
+                square_t(n, 0)
+            root_d2(i, 1, 0)
+            if feed:
+                area_t(m, 1)
+            root_d2(i, 1, 1)
+            power_v(i, 0)
+            if ahead:
+                square_t(n, 1)
+            if not last:
+                square_v(i, 1)
+                speed_v(i, 1)
+                mx(i + 1, 1, 0, range(NW))
+                mx(i + 1, 1, 1, range(NW))
+                if ahead:
+                    turn_o(n)
+                    lay_o(n, 0)
+                    lay_o(n, 1)
+                    lay_o(n, 2)
+                if feed:
+                    quant_t(m)
+                power_v(i, 1)
+                if feed:
+                    quant_o(m)
+            else:
+                for h in range(2):
+                    square_v(i, 1, h * H, (h + 1) * H)
+                    speed_v(i, 1, h * H, (h + 1) * H)
+                    power_v(i, 1, h * H, (h + 1) * H)

@@ -23,6 +23,7 @@ NW = GT + GL
 ROWS = M // P
 PAIRS = ROWS // 2
 H = 512
+Q = 256
 
 
 def tile_wind_farm_wakes_s2_kernel(tc, thrust, area, kern, outer, okern, inflow, speed, power):
@@ -32,17 +33,16 @@ def tile_wind_farm_wakes_s2_kernel(tc, thrust, area, kern, outer, okern, inflow,
         work = ctx.enter_context(tc.tile_pool(name="work", bufs=2))
         turn = ctx.enter_context(tc.psum_pool(name="turn", bufs=4))
         sums = ctx.enter_context(tc.psum_pool(name="sums", bufs=4))
-        ctx.enter_context(tc.manual_schedule())
 
+        area_b = keep.tile([P, GT, 4], BF16, name="area_b")
+        inflow_b = keep.tile([P, ROWS], BF16, name="inflow_b")
+        nc.scalar.dma_start(out=area_b[:], in_=area.rearrange("(g p j) -> p g j", g=GT, j=4))
+        nc.scalar.dma_start(out=inflow_b[:], in_=inflow.rearrange("(p t) -> p t", t=ROWS))
         ident = keep.tile([P, P], F32, name="ident")
         make_identity(nc, ident[:])
         dummy = keep.tile([P, 1], F32, name="dummy")
         nc.gpsimd.memset(dummy[:], 1.0)
         nc.scalar.activation(out=dummy[:], in_=dummy[:], func=ACT.Sqrt)
-        area_b = keep.tile([P, GT, 4], BF16, name="area_b")
-        inflow_b = keep.tile([P, ROWS], BF16, name="inflow_b")
-        nc.scalar.dma_start(out=area_b[:], in_=area.rearrange("(g p j) -> p g j", g=GT, j=4))
-        nc.scalar.dma_start(out=inflow_b[:], in_=inflow.rearrange("(p t) -> p t", t=ROWS))
         inflow_f = keep.tile([P, ROWS], F32, name="inflow_f")
 
         w_hbm = [kern[g * KP:(g + 1) * KP, :] for g in range(GT)] + [okern[g * KP:(g + 1) * KP, :] for g in range(GL)]
@@ -53,17 +53,17 @@ def tile_wind_farm_wakes_s2_kernel(tc, thrust, area, kern, outer, okern, inflow,
         def load_w(w, c0, width):
             raw = keep.tile([P, 4, width], BF16, name="w_raw_%d_%d" % (w, c0), align_bytes=64)
             nc.sync.dma_start(out=raw[:], in_=w_hbm[w].rearrange("(p j) n -> p j n", j=4)[:, :, c0:c0 + width])
-            for h in range(2):
-                if c0 <= h * H < c0 + width:
-                    w_raw[w, h] = raw[:, :, h * H - c0:h * H - c0 + H]
+            for c in range(c0, c0 + width, Q):
+                w_raw[w, c] = raw[:, :, c - c0:]
 
         def load_x(i):
-            t_raw[i] = keep.tile([P, 2, T], BF16, name="t_raw_%d" % i, align_bytes=64)
+            t_raw[i] = work.tile([P, 2, T], BF16, name="t_raw", bufs=3, align_bytes=64)
             nc.sync.dma_start(out=t_raw[i][:], in_=thrust.rearrange("(p t) k -> p t k", t=ROWS)[:, 2 * i:2 * i + 2, :])
-            o_raw[i] = keep.tile([P, 2, L], BF16, name="o_raw_%d" % i, align_bytes=64)
+            o_raw[i] = work.tile([P, 2, L], BF16, name="o_raw", bufs=3, align_bytes=64)
             nc.sync.dma_start(out=o_raw[i][:], in_=outer.rearrange("(p t) k -> p t k", t=ROWS)[:, 2 * i:2 * i + 2, :])
 
-        load_w(0, 0, H)
+        load_w(0, 0, Q)
+        load_w(0, Q, Q)
         load_w(0, H, H)
         load_x(0)
         load_w(1, 0, N)
@@ -72,18 +72,17 @@ def tile_wind_farm_wakes_s2_kernel(tc, thrust, area, kern, outer, okern, inflow,
         load_w(3, 0, N)
         load_w(4, 0, N)
         load_x(2)
-        load_x(3)
 
         w_codes = [keep.tile([P, N], U32, name="w_codes_%d" % w, align_bytes=64) for w in range(NW)]
         w_scales = [keep.tile([P, N], U8, name="w_scales_%d" % w, align_bytes=64) for w in range(NW)]
         w_lay = {}
 
-        def lay(w, h, copy):
-            dst = work.tile([P, H, 4], BF16, name="w_lay", bufs=3, align_bytes=64)
-            w_lay[w, h] = dst
+        def lay(w, h, copy, c0=0, c1=H):
+            if c0 == 0:
+                w_lay[w, h] = work.tile([P, H, 4], BF16, name="w_lay", bufs=5, align_bytes=64)
             copy(
-                out=dst[:].rearrange("p (c i) j -> p c j i", i=4),
-                in_=w_raw[w, h].rearrange("p j (c i) -> p c j i", i=4),
+                out=w_lay[w, h][:, c0:c1].rearrange("p (c i) j -> p c j i", i=4),
+                in_=w_raw[w, h * H + c0][:, :, 0:c1 - c0].rearrange("p j (c i) -> p c j i", i=4),
             )
 
         def quant_w(w, h):
@@ -152,10 +151,10 @@ def tile_wind_farm_wakes_s2_kernel(tc, thrust, area, kern, outer, okern, inflow,
                 in_=t_a[i][:].rearrange("p g c j -> p (g c j)"),
             )
 
-        def lay_o(i, g):
+        def lay_o(i, g, copy):
             if g == 0:
                 o_lay[i] = work.tile([P, GL, 2 * P, 2], F32, name="o_lay", bufs=2, align_bytes=64)
-            nc.scalar.copy(out=o_lay[i][:, g], in_=banks["o", i, g][:].rearrange("p u c -> p c u"))
+            copy(out=o_lay[i][:, g], in_=banks["o", i, g][:].rearrange("p u c -> p c u"))
 
         def quant_o(i):
             src = o_lay[i][:].rearrange("p g c u -> p g (c u)").bitcast(BF16)
@@ -196,7 +195,7 @@ def tile_wind_farm_wakes_s2_kernel(tc, thrust, area, kern, outer, okern, inflow,
 
         def root_d2(i, mt, h):
             if h == 0:
-                root[i, mt] = work.tile([P, N], F32, name="root", bufs=2)
+                root[i, mt] = work.tile([P, N], F32, name="root", bufs=3)
             nc.scalar.activation(out=root[i, mt][:, h * H:(h + 1) * H], in_=acc[i, mt, h][:], func=ACT.Sqrt)
 
         def square_v(i, mt, c0=0, c1=N):
@@ -217,6 +216,11 @@ def tile_wind_farm_wakes_s2_kernel(tc, thrust, area, kern, outer, okern, inflow,
             )
             nc.sync.dma_start(out=speed.rearrange("(p t) n -> p t n", t=ROWS)[:, r, c0:c1], in_=vel[i, mt][:, c0:c1])
 
+        def square_dve(i, mt, c0, c1):
+            nc.vector.tensor_tensor(
+                out=vel2[i, mt][:, c0:c1], in0=vel[i, mt][:, c0:c1], in1=vel[i, mt][:, c0:c1], op=ALU.mult
+            )
+
         def power_v(i, mt, c0=0, c1=N):
             r = 2 * i + mt
             if c0 == 0:
@@ -229,105 +233,91 @@ def tile_wind_farm_wakes_s2_kernel(tc, thrust, area, kern, outer, okern, inflow,
         act_copy = nc.scalar.copy
         dve_copy = nc.vector.tensor_copy
 
-        lay(0, 0, act_copy)
-        nc.vector.tensor_copy(out=inflow_f[:], in_=inflow_b[:])
+        lay(0, 0, act_copy, 0, Q)
+        lay(0, 0, dve_copy, Q, H)
         lay(0, 1, dve_copy)
         turn_t(0)
         square_t(0, 0)
+        square_t(0, 1)
         quant_w(0, 0)
         quant_w(0, 1)
-        square_t(0, 1)
         area_t(0, 0)
-        turn_o(0)
-        lay_o(0, 0)
-        lay_o(0, 1)
-        lay_o(0, 2)
         area_t(0, 1)
-        lay(1, 1, dve_copy)
+        turn_o(0)
+        load_x(3)
+        for g in range(GL):
+            lay_o(0, g, act_copy)
         lay(1, 0, act_copy)
+        lay(1, 1, dve_copy)
         quant_t(0)
-        quant_o(0)
         lay(2, 1, dve_copy)
-        quant_w(1, 1)
-        quant_w(1, 0)
+        quant_o(0)
         mx_all(0, [0])
-        lay(2, 0, act_copy)
-        quant_w(2, 1)
         turn_t(1)
-        mx_all(0, [1])
+        lay(2, 0, act_copy)
+        quant_w(1, 1)
+        nc.vector.tensor_copy(out=inflow_f[:], in_=inflow_b[:])
+        quant_w(1, 0)
+        quant_w(2, 1)
         square_t(1, 0)
         square_t(1, 1)
-        quant_w(2, 0)
-        area_t(1, 0)
         turn_o(1)
-        lay_o(1, 0)
-        lay_o(1, 1)
-        lay_o(1, 2)
+        mx_all(0, [1])
+        for g in range(GL):
+            lay_o(1, g, act_copy)
+        quant_w(2, 0)
         lay(3, 1, dve_copy)
+        area_t(1, 0)
         area_t(1, 1)
         mx_all(0, [2])
-        lay(3, 0, act_copy)
-        quant_w(3, 1)
-        quant_t(1)
-        lay(4, 0, dve_copy)
-        quant_o(1)
-        quant_w(3, 0)
-        lay(4, 1, dve_copy)
-        quant_w(4, 0)
         turn_t(2)
+        lay(3, 0, act_copy)
+        lay(4, 1, dve_copy)
+        quant_t(1)
+        quant_w(3, 1)
+        quant_o(1)
+        lay(4, 0, act_copy)
+        quant_w(3, 0)
+        quant_w(4, 1)
         square_t(2, 0)
         square_t(2, 1)
         turn_o(2)
-        lay_o(2, 0)
-        lay_o(2, 1)
-        lay_o(2, 2)
-        area_t(2, 0)
-        quant_w(4, 1)
-        mx_all(0, [3, 4])
+        for g in range(GL):
+            lay_o(2, g, act_copy)
+        mx_all(0, [3])
+        quant_w(4, 0)
+        mx_all(0, [4])
 
-        for i in range(PAIRS):
-            n = i + 3
+        for r in range(ROWS):
+            i, mt = divmod(r, 2)
             m = i + 2
-            ahead = n < PAIRS
-            feed = m < PAIRS
-            last = i == PAIRS - 1
-            root_d2(i, 0, 0)
-            root_d2(i, 0, 1)
-            if ahead:
-                turn_t(n)
-            if feed and i > 0:
-                area_t(m, 0)
-            if not last:
-                mx(i + 1, 0, 0, range(NW))
-                mx(i + 1, 0, 1, range(NW))
-            square_v(i, 0)
-            speed_v(i, 0)
-            if ahead:
-                square_t(n, 0)
-            root_d2(i, 1, 0)
-            if feed:
-                area_t(m, 1)
-            root_d2(i, 1, 1)
-            power_v(i, 0)
-            if ahead:
-                square_t(n, 1)
-            if not last:
-                square_v(i, 1)
-                speed_v(i, 1)
-                mx(i + 1, 1, 0, range(NW))
-                mx(i + 1, 1, 1, range(NW))
-                if ahead:
+            n = i + 3
+            if n < PAIRS:
+                if mt == 0:
+                    turn_t(n)
+                else:
                     turn_o(n)
-                    lay_o(n, 0)
-                    lay_o(n, 1)
-                    lay_o(n, 2)
-                if feed:
-                    quant_t(m)
-                power_v(i, 1)
-                if feed:
-                    quant_o(m)
-            else:
-                for h in range(2):
-                    square_v(i, 1, h * H, (h + 1) * H)
-                    speed_v(i, 1, h * H, (h + 1) * H)
-                    power_v(i, 1, h * H, (h + 1) * H)
+            root_d2(i, mt, 0)
+            root_d2(i, mt, 1)
+            if r + 2 < ROWS:
+                mx(i + 1, mt, 0, range(NW))
+                mx(i + 1, mt, 1, range(NW))
+            if n < PAIRS and mt == 0:
+                square_t(n, 0)
+                square_t(n, 1)
+            if n < PAIRS and mt == 1:
+                for g in range(GL):
+                    lay_o(n, g, act_copy)
+            if m < PAIRS and mt == 0:
+                area_t(m, 0)
+                area_t(m, 1)
+            if m < PAIRS and mt == 1:
+                quant_t(m)
+                quant_o(m)
+            speed_v(i, mt)
+            if r > 0:
+                square_v((r - 1) // 2, (r - 1) % 2)
+                power_v((r - 1) // 2, (r - 1) % 2)
+        for h in range(2):
+            square_v(PAIRS - 1, 1, h * H, (h + 1) * H)
+            power_v(PAIRS - 1, 1, h * H, (h + 1) * H)

@@ -34,6 +34,7 @@ def tile_wind_farm_wakes_s2_kernel(tc, thrust, area, kern, outer, okern, inflow,
         turn = ctx.enter_context(tc.psum_pool(name="turn", bufs=4))
         sums = ctx.enter_context(tc.psum_pool(name="sums", bufs=4))
 
+        ctx.enter_context(tc.manual_schedule())
         area_b = keep.tile([P, GT, 4], BF16, name="area_b")
         inflow_b = keep.tile([P, ROWS], BF16, name="inflow_b")
         nc.scalar.dma_start(out=area_b[:], in_=area.rearrange("(g p j) -> p g j", g=GT, j=4))
@@ -79,7 +80,7 @@ def tile_wind_farm_wakes_s2_kernel(tc, thrust, area, kern, outer, okern, inflow,
 
         def lay(w, h, copy, c0=0, c1=H):
             if c0 == 0:
-                w_lay[w, h] = work.tile([P, H, 4], BF16, name="w_lay", bufs=5, align_bytes=64)
+                w_lay[w, h] = work.tile([P, H, 4], BF16, name="w_lay", bufs=4, align_bytes=64)
             copy(
                 out=w_lay[w, h][:, c0:c1].rearrange("p (c i) j -> p c j i", i=4),
                 in_=w_raw[w, h * H + c0][:, :, 0:c1 - c0].rearrange("p j (c i) -> p c j i", i=4),
@@ -209,7 +210,7 @@ def tile_wind_farm_wakes_s2_kernel(tc, thrust, area, kern, outer, okern, inflow,
         def speed_v(i, mt, c0=0, c1=N):
             r = 2 * i + mt
             if c0 == 0:
-                vel[i, mt] = work.tile([P, N], F32, name="vel", bufs=3)
+                vel[i, mt] = work.tile([P, N], F32, name="vel", bufs=4)
             nc.vector.tensor_scalar(
                 out=vel[i, mt][:, c0:c1], in0=root[i, mt][:, c0:c1], scalar1=-1.0, scalar2=inflow_f[:, r:r + 1],
                 op0=ALU.mult, op1=ALU.add,
@@ -224,7 +225,7 @@ def tile_wind_farm_wakes_s2_kernel(tc, thrust, area, kern, outer, okern, inflow,
         def power_v(i, mt, c0=0, c1=N):
             r = 2 * i + mt
             if c0 == 0:
-                pw[i, mt] = work.tile([P, N], F32, name="pw", bufs=3)
+                pw[i, mt] = work.tile([P, N], F32, name="pw", bufs=4)
             nc.vector.tensor_tensor(
                 out=pw[i, mt][:, c0:c1], in0=vel2[i, mt][:, c0:c1], in1=vel[i, mt][:, c0:c1], op=ALU.mult
             )
@@ -276,7 +277,7 @@ def tile_wind_farm_wakes_s2_kernel(tc, thrust, area, kern, outer, okern, inflow,
         quant_t(1)
         quant_w(3, 1)
         quant_o(1)
-        lay(4, 0, act_copy)
+        lay(4, 0, dve_copy)
         quant_w(3, 0)
         quant_w(4, 1)
         square_t(2, 0)
@@ -284,40 +285,44 @@ def tile_wind_farm_wakes_s2_kernel(tc, thrust, area, kern, outer, okern, inflow,
         turn_o(2)
         for g in range(GL):
             lay_o(2, g, act_copy)
+        turn_t(3)
         mx_all(0, [3])
         quant_w(4, 0)
         mx_all(0, [4])
+        square_t(3, 0)
 
         for r in range(ROWS):
             i, mt = divmod(r, 2)
             m = i + 2
-            n = i + 3
-            if n < PAIRS:
-                if mt == 0:
-                    turn_t(n)
-                else:
-                    turn_o(n)
+            if r == 1:
+                turn_o(3)
             root_d2(i, mt, 0)
             root_d2(i, mt, 1)
             if r + 2 < ROWS:
                 mx(i + 1, mt, 0, range(NW))
                 mx(i + 1, mt, 1, range(NW))
-            if n < PAIRS and mt == 0:
-                square_t(n, 0)
-                square_t(n, 1)
-            if n < PAIRS and mt == 1:
-                for g in range(GL):
-                    lay_o(n, g, act_copy)
-            if m < PAIRS and mt == 0:
-                area_t(m, 0)
-                area_t(m, 1)
-            if m < PAIRS and mt == 1:
-                quant_t(m)
-                quant_o(m)
+            if r == 0:
+                square_t(3, 1)
+            if r == 1:
+                lay_o(3, 0, act_copy)
+            if m < PAIRS:
+                if mt == 0:
+                    area_t(m, 0)
+                else:
+                    quant_t(m)
             speed_v(i, mt)
-            if r > 0:
-                square_v((r - 1) // 2, (r - 1) % 2)
-                power_v((r - 1) // 2, (r - 1) % 2)
+            if r < ROWS - 1:
+                square_v(i, mt)
+            if m < PAIRS:
+                if mt == 0:
+                    area_t(m, 1)
+                else:
+                    quant_o(m)
+            if r == 1:
+                lay_o(3, 1, act_copy)
+                lay_o(3, 2, act_copy)
+            if r < ROWS - 1:
+                power_v(i, mt)
         for h in range(2):
             square_v(PAIRS - 1, 1, h * H, (h + 1) * H)
             power_v(PAIRS - 1, 1, h * H, (h + 1) * H)

@@ -31,8 +31,8 @@ def tile_wind_farm_wakes_s2_kernel(tc, thrust, area, kern, outer, okern, inflow,
     with ExitStack() as ctx:
         keep = ctx.enter_context(tc.tile_pool(name="keep", bufs=1))
         work = ctx.enter_context(tc.tile_pool(name="work", bufs=2))
-        turn = ctx.enter_context(tc.psum_pool(name="turn", bufs=4))
-        sums = ctx.enter_context(tc.psum_pool(name="sums", bufs=4))
+        turn = ctx.enter_context(tc.psum_pool(name="turn", bufs=2))
+        sums = ctx.enter_context(tc.psum_pool(name="sums", bufs=6))
 
         ctx.enter_context(tc.manual_schedule())
         area_b = keep.tile([P, GT, 4], BF16, name="area_b")
@@ -57,32 +57,23 @@ def tile_wind_farm_wakes_s2_kernel(tc, thrust, area, kern, outer, okern, inflow,
             for c in range(c0, c0 + width, Q):
                 w_raw[w, c] = raw[:, :, c - c0:]
 
-        def load_x(i):
+        def load_t(i):
             t_raw[i] = work.tile([P, 2, T], BF16, name="t_raw", bufs=3, align_bytes=64)
             nc.sync.dma_start(out=t_raw[i][:], in_=thrust.rearrange("(p t) k -> p t k", t=ROWS)[:, 2 * i:2 * i + 2, :])
+
+        def load_o(i):
             o_raw[i] = work.tile([P, 2, L], BF16, name="o_raw", bufs=3, align_bytes=64)
             nc.sync.dma_start(out=o_raw[i][:], in_=outer.rearrange("(p t) k -> p t k", t=ROWS)[:, 2 * i:2 * i + 2, :])
-
-        load_w(0, 0, Q)
-        load_w(0, Q, Q)
-        load_w(0, H, H)
-        load_x(0)
-        load_w(1, 0, N)
-        load_w(2, 0, N)
-        load_x(1)
-        load_w(3, 0, N)
-        load_w(4, 0, N)
-        load_x(2)
 
         w_codes = [keep.tile([P, N], U32, name="w_codes_%d" % w, align_bytes=64) for w in range(NW)]
         w_scales = [keep.tile([P, N], U8, name="w_scales_%d" % w, align_bytes=64) for w in range(NW)]
         w_lay = {}
 
         def lay(w, h, copy, c0=0, c1=H):
-            if c0 == 0:
-                w_lay[w, h] = work.tile([P, H, 4], BF16, name="w_lay", bufs=4, align_bytes=64)
+            if (w, 0) not in w_lay:
+                w_lay[w, 0] = work.tile([P, N, 4], BF16, name="w_lay", bufs=3, align_bytes=64)
             copy(
-                out=w_lay[w, h][:, c0:c1].rearrange("p (c i) j -> p c j i", i=4),
+                out=w_lay[w, 0][:, h * H + c0:h * H + c1].rearrange("p (c i) j -> p c j i", i=4),
                 in_=w_raw[w, h * H + c0][:, :, 0:c1 - c0].rearrange("p j (c i) -> p c j i", i=4),
             )
 
@@ -91,7 +82,7 @@ def tile_wind_farm_wakes_s2_kernel(tc, thrust, area, kern, outer, okern, inflow,
             nc.vector.quantize_mx(
                 out=w_codes[w][:, cols].bitcast(E4M3),
                 scales=w_scales[w][:, cols],
-                in_=w_lay[w, h][:].rearrange("p c j -> p (c j)"),
+                in_=w_lay[w, 0][:, cols].rearrange("p c j -> p (c j)"),
             )
 
         x_codes = {}
@@ -114,20 +105,19 @@ def tile_wind_farm_wakes_s2_kernel(tc, thrust, area, kern, outer, okern, inflow,
                     )
             return bank
 
+        def turn_t(i, g):
+            banks["t", i, g] = turn_x(t_raw[i], g)
+
+        def turn_o(i, g):
+            banks["o", i, g] = turn_x(o_raw[i], g)
+
         t_sq = {}
         t_a = {}
         o_lay = {}
 
-        def turn_t(i):
-            for g in range(GT):
-                banks["t", i, g] = turn_x(t_raw[i], g)
-
-        def turn_o(i):
-            for g in range(GL):
-                banks["o", i, g] = turn_x(o_raw[i], g)
 
         def square_t(i, g):
-            if g == 0:
+            if i not in t_sq:
                 t_sq[i] = work.tile([P, GT, 2 * P, 4], F32, name="t_sq", bufs=2, align_bytes=64)
             nc.scalar.activation(
                 out=t_sq[i][:, g].rearrange("p c (u e) -> p c u e", e=2),
@@ -136,13 +126,20 @@ def tile_wind_farm_wakes_s2_kernel(tc, thrust, area, kern, outer, okern, inflow,
             )
 
         def area_t(i, g):
-            if g == 0:
+            if i not in t_a:
                 t_a[i] = work.tile([P, GT, 2 * P, 4], BF16, name="t_a", bufs=2, align_bytes=64)
             nc.vector.tensor_tensor(
                 out=t_a[i][:, g],
                 in0=t_sq[i][:, g],
                 in1=area_b[:, g, :].unsqueeze(1).to_broadcast([P, 2 * P, 4]),
                 op=ALU.mult,
+            )
+
+        def quant_w2(w):
+            nc.vector.quantize_mx(
+                out=w_codes[w][:].bitcast(E4M3),
+                scales=w_scales[w][:],
+                in_=w_lay[w, 0][:].rearrange("p c j -> p (c j)"),
             )
 
         def quant_t(i):
@@ -153,13 +150,13 @@ def tile_wind_farm_wakes_s2_kernel(tc, thrust, area, kern, outer, okern, inflow,
             )
 
         def lay_o(i, g, copy):
-            if g == 0:
+            if i not in o_lay:
                 o_lay[i] = work.tile([P, GL, 2 * P, 2], F32, name="o_lay", bufs=2, align_bytes=64)
             copy(out=o_lay[i][:, g], in_=banks["o", i, g][:].rearrange("p u c -> p c u"))
 
-        def quant_o(i):
+        def quant_o(i, part):
             src = o_lay[i][:].rearrange("p g c u -> p g (c u)").bitcast(BF16)
-            for g0, g1 in ((0, 2), (2, 3)):
+            for g0, g1 in (((0, 2), (2, 3))[part],):
                 nc.vector.quantize_mx(
                     out=x_codes[i][:, GT + g0:GT + g1, :].rearrange("p g c -> p (g c)").bitcast(E4M3),
                     scales=x_scales[i][:, GT + g0:GT + g1, :].rearrange("p g c -> p (g c)"),
@@ -169,7 +166,7 @@ def tile_wind_farm_wakes_s2_kernel(tc, thrust, area, kern, outer, okern, inflow,
         acc = {}
 
         def mx(i, mt, h, passes):
-            if 0 in passes:
+            if (i, mt, h) not in acc:
                 acc[i, mt, h] = sums.tile([P, H], F32, name="acc")
             rows = slice(mt * P, (mt + 1) * P)
             cols = slice(h * H, (h + 1) * H)
@@ -195,13 +192,13 @@ def tile_wind_farm_wakes_s2_kernel(tc, thrust, area, kern, outer, okern, inflow,
         pw = {}
 
         def root_d2(i, mt, h):
-            if h == 0:
+            if (i, mt) not in root:
                 root[i, mt] = work.tile([P, N], F32, name="root", bufs=3)
             nc.scalar.activation(out=root[i, mt][:, h * H:(h + 1) * H], in_=acc[i, mt, h][:], func=ACT.Sqrt)
 
         def square_v(i, mt, c0=0, c1=N):
             r = 2 * i + mt
-            if c0 == 0:
+            if (i, mt) not in vel2:
                 vel2[i, mt] = work.tile([P, N], F32, name="vel2", bufs=2)
             nc.scalar.activation(
                 out=vel2[i, mt][:, c0:c1], in_=root[i, mt][:, c0:c1], func=ACT.Square, scale=-1.0, bias=inflow_f[:, r:r + 1]
@@ -209,7 +206,7 @@ def tile_wind_farm_wakes_s2_kernel(tc, thrust, area, kern, outer, okern, inflow,
 
         def speed_v(i, mt, c0=0, c1=N):
             r = 2 * i + mt
-            if c0 == 0:
+            if (i, mt) not in vel:
                 vel[i, mt] = work.tile([P, N], F32, name="vel", bufs=4)
             nc.vector.tensor_scalar(
                 out=vel[i, mt][:, c0:c1], in0=root[i, mt][:, c0:c1], scalar1=-1.0, scalar2=inflow_f[:, r:r + 1],
@@ -224,7 +221,7 @@ def tile_wind_farm_wakes_s2_kernel(tc, thrust, area, kern, outer, okern, inflow,
 
         def power_v(i, mt, c0=0, c1=N):
             r = 2 * i + mt
-            if c0 == 0:
+            if (i, mt) not in pw:
                 pw[i, mt] = work.tile([P, N], F32, name="pw", bufs=4)
             nc.vector.tensor_tensor(
                 out=pw[i, mt][:, c0:c1], in0=vel2[i, mt][:, c0:c1], in1=vel[i, mt][:, c0:c1], op=ALU.mult
@@ -234,95 +231,196 @@ def tile_wind_farm_wakes_s2_kernel(tc, thrust, area, kern, outer, okern, inflow,
         act_copy = nc.scalar.copy
         dve_copy = nc.vector.tensor_copy
 
-        lay(0, 0, act_copy, 0, Q)
-        lay(0, 0, dve_copy, Q, H)
-        lay(0, 1, dve_copy)
-        turn_t(0)
+        load_t(0)
+        load_w(0, 512, 512)
+        turn_t(0, 0)
         square_t(0, 0)
+        turn_t(0, 1)
+        lay(0, 1, dve_copy)
+        load_o(0)
+        load_w(0, 256, 256)
+        load_w(1, 0, 1024)
+        load_t(1)
+        turn_o(0, 2)
+        load_w(0, 0, 256)
         square_t(0, 1)
-        quant_w(0, 0)
-        quant_w(0, 1)
         area_t(0, 0)
         area_t(0, 1)
-        turn_o(0)
-        load_x(3)
-        for g in range(GL):
-            lay_o(0, g, act_copy)
-        lay(1, 0, act_copy)
-        lay(1, 1, dve_copy)
+        lay_o(0, 2, act_copy)
+        turn_o(0, 1)
+        quant_w(0, 1)
         quant_t(0)
-        lay(2, 1, dve_copy)
-        quant_o(0)
-        mx_all(0, [0])
-        turn_t(1)
-        lay(2, 0, act_copy)
-        quant_w(1, 1)
-        nc.vector.tensor_copy(out=inflow_f[:], in_=inflow_b[:])
-        quant_w(1, 0)
-        quant_w(2, 1)
+        lay(0, 0, act_copy, 256, 512)
+        lay_o(0, 1, dve_copy)
+        turn_o(0, 0)
+        mx(0, 0, 1, [0])
+        lay_o(0, 0, act_copy)
+        load_w(2, 0, 1024)
+        load_o(1)
+        lay(1, 1, dve_copy)
+        load_t(2)
+        lay(1, 0, act_copy)
+        turn_t(1, 0)
         square_t(1, 0)
+        turn_t(1, 1)
         square_t(1, 1)
-        turn_o(1)
-        mx_all(0, [1])
-        for g in range(GL):
-            lay_o(1, g, act_copy)
-        quant_w(2, 0)
-        lay(3, 1, dve_copy)
+        lay(0, 0, dve_copy, 0, 256)
+        quant_w(0, 0)
+        nc.vector.tensor_copy(out=inflow_f[:], in_=inflow_b[:])
+        quant_o(0, 0)
+        mx(0, 0, 0, [0])
+        mx(0, 1, 0, [0])
+        turn_o(1, 1)
+        turn_o(1, 0)
         area_t(1, 0)
         area_t(1, 1)
-        mx_all(0, [2])
-        turn_t(2)
-        lay(3, 0, act_copy)
-        lay(4, 1, dve_copy)
+        lay_o(1, 1, dve_copy)
+        turn_o(1, 2)
+        lay(2, 1, act_copy)
+        lay_o(1, 0, act_copy)
+        lay_o(1, 2, act_copy)
+        turn_t(2, 1)
+        load_t(3)
+        turn_t(3, 0)
+        load_w(3, 0, 1024)
+        quant_w2(1)
+        mx(0, 1, 1, [0, 1])
+        mx(0, 0, 1, [1])
+        lay(2, 0, dve_copy)
+        load_o(2)
+        load_w(4, 0, 1024)
+        load_o(3)
         quant_t(1)
-        quant_w(3, 1)
-        quant_o(1)
-        lay(4, 0, dve_copy)
-        quant_w(3, 0)
-        quant_w(4, 1)
-        square_t(2, 0)
+        mx(0, 1, 0, [1])
+        quant_w2(2)
+        lay(3, 0, dve_copy)
+        mx(1, 1, 0, [0, 1])
         square_t(2, 1)
-        turn_o(2)
-        for g in range(GL):
-            lay_o(2, g, act_copy)
-        turn_t(3)
-        mx_all(0, [3])
-        quant_w(4, 0)
-        mx_all(0, [4])
+        quant_o(0, 1)
         square_t(3, 0)
-
-        for r in range(ROWS):
-            i, mt = divmod(r, 2)
-            m = i + 2
-            if r == 1:
-                turn_o(3)
-            root_d2(i, mt, 0)
-            root_d2(i, mt, 1)
-            if r + 2 < ROWS:
-                mx(i + 1, mt, 0, range(NW))
-                mx(i + 1, mt, 1, range(NW))
-            if r == 0:
-                square_t(3, 1)
-            if r == 1:
-                lay_o(3, 0, act_copy)
-            if m < PAIRS:
-                if mt == 0:
-                    area_t(m, 0)
-                else:
-                    quant_t(m)
-            speed_v(i, mt)
-            if r < ROWS - 1:
-                square_v(i, mt)
-            if m < PAIRS:
-                if mt == 0:
-                    area_t(m, 1)
-                else:
-                    quant_o(m)
-            if r == 1:
-                lay_o(3, 1, act_copy)
-                lay_o(3, 2, act_copy)
-            if r < ROWS - 1:
-                power_v(i, mt)
-        for h in range(2):
-            square_v(PAIRS - 1, 1, h * H, (h + 1) * H)
-            power_v(PAIRS - 1, 1, h * H, (h + 1) * H)
+        lay(3, 1, act_copy)
+        quant_o(1, 0)
+        quant_w2(3)
+        turn_t(2, 0)
+        mx(0, 0, 0, [1, 2])
+        square_t(2, 0)
+        lay(4, 1, act_copy)
+        mx(0, 0, 1, [2])
+        lay(4, 0, dve_copy)
+        area_t(2, 0)
+        quant_w2(4)
+        mx(1, 0, 0, [0, 1])
+        quant_o(1, 1)
+        mx(0, 1, 0, [2])
+        mx(0, 1, 1, [2])
+        turn_o(2, 2)
+        turn_o(2, 1)
+        lay_o(2, 2, act_copy)
+        mx(0, 0, 1, [3])
+        mx(0, 0, 0, [3])
+        mx(0, 1, 0, [3])
+        lay_o(2, 1, act_copy)
+        mx(0, 1, 1, [3])
+        mx(1, 1, 0, [2])
+        mx(1, 0, 0, [2])
+        mx(1, 1, 0, [3])
+        turn_t(3, 1)
+        quant_o(2, 1)
+        area_t(2, 1)
+        turn_o(2, 0)
+        mx(0, 0, 1, [4])
+        mx(1, 0, 0, [3])
+        mx(0, 0, 0, [4])
+        square_t(3, 1)
+        root_d2(0, 0, 1)
+        mx(0, 1, 0, [4])
+        root_d2(0, 0, 0)
+        area_t(3, 1)
+        speed_v(0, 0)
+        quant_t(2)
+        mx(0, 1, 1, [4])
+        root_d2(0, 1, 0)
+        mx(1, 1, 1, [0])
+        square_v(0, 0)
+        power_v(0, 0)
+        area_t(3, 0)
+        turn_o(3, 1)
+        mx(1, 0, 1, [0])
+        lay_o(3, 1, act_copy)
+        mx(1, 1, 0, [4])
+        lay_o(2, 0, act_copy)
+        mx(1, 1, 1, [1, 2])
+        root_d2(0, 1, 1)
+        mx(1, 0, 0, [4])
+        root_d2(1, 0, 0)
+        square_v(0, 1)
+        mx(1, 1, 1, [3])
+        mx(2, 1, 1, [0])
+        mx(1, 0, 1, [1])
+        speed_v(0, 1)
+        quant_o(2, 0)
+        power_v(0, 1)
+        mx(1, 0, 1, [2, 3, 4])
+        mx(1, 1, 1, [4])
+        turn_o(3, 2)
+        lay_o(3, 2, dve_copy)
+        turn_o(3, 0)
+        mx(2, 0, 0, [0])
+        root_d2(1, 0, 1)
+        speed_v(1, 0)
+        root_d2(1, 1, 0)
+        root_d2(1, 1, 1)
+        speed_v(1, 1)
+        mx(2, 0, 1, [0])
+        mx(2, 0, 0, [1, 2])
+        lay_o(3, 0, act_copy)
+        mx(2, 0, 0, [3, 4])
+        mx(2, 1, 0, [0])
+        mx(2, 1, 1, [1])
+        root_d2(2, 0, 0)
+        mx(2, 0, 1, [1, 2, 3, 4])
+        quant_t(3)
+        square_v(1, 0)
+        root_d2(2, 0, 1)
+        square_v(2, 0)
+        mx(2, 1, 0, [1])
+        quant_o(3, 0)
+        power_v(1, 0)
+        speed_v(2, 0)
+        quant_o(3, 1)
+        mx(2, 1, 0, [2, 3, 4])
+        mx(3, 0, 1, [0, 1])
+        mx(3, 0, 0, [0, 1])
+        mx(2, 1, 1, [2])
+        root_d2(2, 1, 0)
+        square_v(1, 1)
+        mx(2, 1, 1, [3, 4])
+        root_d2(2, 1, 1)
+        power_v(2, 0)
+        power_v(1, 1)
+        speed_v(2, 1)
+        mx(3, 0, 1, [2])
+        mx(3, 0, 0, [2])
+        mx(3, 0, 1, [3, 4])
+        mx(3, 0, 0, [3])
+        root_d2(3, 0, 1)
+        mx(3, 0, 0, [4])
+        root_d2(3, 0, 0)
+        mx(3, 1, 1, [0, 1])
+        square_v(3, 0)
+        square_v(2, 1)
+        mx(3, 1, 0, [0, 1, 2])
+        mx(3, 1, 1, [2, 3, 4])
+        mx(3, 1, 0, [3])
+        speed_v(3, 0)
+        power_v(3, 0)
+        root_d2(3, 1, 1)
+        mx(3, 1, 0, [4])
+        square_v(3, 1, 512, 1024)
+        root_d2(3, 1, 0)
+        power_v(2, 1)
+        speed_v(3, 1, 512, 1024)
+        speed_v(3, 1, 0, 512)
+        square_v(3, 1, 0, 512)
+        power_v(3, 1, 0, 512)
+        power_v(3, 1, 512, 1024)

@@ -31,10 +31,9 @@ def tile_wind_farm_wakes_s2_kernel(tc, thrust, area, kern, outer, okern, inflow,
     with ExitStack() as ctx:
         keep = ctx.enter_context(tc.tile_pool(name="keep", bufs=1))
         work = ctx.enter_context(tc.tile_pool(name="work", bufs=2))
-        turn = ctx.enter_context(tc.psum_pool(name="turn", bufs=2))
-        sums = ctx.enter_context(tc.psum_pool(name="sums", bufs=6))
+        turn = ctx.enter_context(tc.psum_pool(name="turn", bufs=4))
+        sums = ctx.enter_context(tc.psum_pool(name="sums", bufs=4))
 
-        ctx.enter_context(tc.manual_schedule())
         area_b = keep.tile([P, GT, 4], BF16, name="area_b")
         inflow_b = keep.tile([P, ROWS], BF16, name="inflow_b")
         nc.scalar.dma_start(out=area_b[:], in_=area.rearrange("(g p j) -> p g j", g=GT, j=4))
@@ -231,196 +230,127 @@ def tile_wind_farm_wakes_s2_kernel(tc, thrust, area, kern, outer, okern, inflow,
         act_copy = nc.scalar.copy
         dve_copy = nc.vector.tensor_copy
 
+        load_w(0, 0, H)
         load_t(0)
-        load_w(0, 512, 512)
-        turn_t(0, 0)
-        square_t(0, 0)
-        turn_t(0, 1)
-        lay(0, 1, dve_copy)
+        load_w(0, H, H)
         load_o(0)
-        load_w(0, 256, 256)
-        load_w(1, 0, 1024)
+        load_w(1, 0, N)
         load_t(1)
-        turn_o(0, 2)
-        load_w(0, 0, 256)
+        load_w(2, 0, N)
+        load_w(3, 0, N)
+        load_o(1)
+        load_w(4, 0, N)
+        load_t(2)
+        load_o(2)
+
+        lay(0, 0, act_copy, 0, Q)
+        lay(0, 0, dve_copy, Q, H)
+        turn_t(0, 0)
+        turn_t(0, 1)
+        square_t(0, 0)
         square_t(0, 1)
+        quant_w(0, 0)
+        lay(0, 1, dve_copy)
+        turn_o(0, 0)
+        turn_o(0, 1)
+        turn_o(0, 2)
+        lay_o(0, 0, act_copy)
+        lay_o(0, 1, act_copy)
         area_t(0, 0)
         area_t(0, 1)
         lay_o(0, 2, act_copy)
-        turn_o(0, 1)
         quant_w(0, 1)
-        quant_t(0)
-        lay(0, 0, act_copy, 256, 512)
-        lay_o(0, 1, dve_copy)
-        turn_o(0, 0)
-        mx(0, 0, 1, [0])
-        lay_o(0, 0, act_copy)
-        load_w(2, 0, 1024)
-        load_o(1)
-        lay(1, 1, dve_copy)
-        load_t(2)
-        lay(1, 0, act_copy)
+        lay(1, 1, act_copy)
+        lay(1, 0, dve_copy)
         turn_t(1, 0)
-        square_t(1, 0)
         turn_t(1, 1)
-        square_t(1, 1)
-        lay(0, 0, dve_copy, 0, 256)
-        quant_w(0, 0)
-        nc.vector.tensor_copy(out=inflow_f[:], in_=inflow_b[:])
+        square_t(1, 0)
+        quant_t(0)
         quant_o(0, 0)
-        mx(0, 0, 0, [0])
-        mx(0, 1, 0, [0])
-        turn_o(1, 1)
-        turn_o(1, 0)
-        area_t(1, 0)
-        area_t(1, 1)
-        lay_o(1, 1, dve_copy)
-        turn_o(1, 2)
-        lay(2, 1, act_copy)
-        lay_o(1, 0, act_copy)
-        lay_o(1, 2, act_copy)
-        turn_t(2, 1)
-        load_t(3)
-        turn_t(3, 0)
-        load_w(3, 0, 1024)
-        quant_w2(1)
-        mx(0, 1, 1, [0, 1])
-        mx(0, 0, 1, [1])
-        lay(2, 0, dve_copy)
-        load_o(2)
-        load_w(4, 0, 1024)
-        load_o(3)
-        quant_t(1)
-        mx(0, 1, 0, [1])
-        quant_w2(2)
-        lay(3, 0, dve_copy)
-        mx(1, 1, 0, [0, 1])
-        square_t(2, 1)
         quant_o(0, 1)
-        square_t(3, 0)
-        lay(3, 1, act_copy)
-        quant_o(1, 0)
-        quant_w2(3)
+        quant_w2(1)
+        for w in range(2):
+            mx_all(0, [w])
+
+        lay(2, 0, dve_copy)
+        lay(2, 1, act_copy)
+        square_t(1, 1)
+        turn_o(1, 0)
+        turn_o(1, 1)
+        turn_o(1, 2)
+        load_t(3)
+        load_o(3)
         turn_t(2, 0)
-        mx(0, 0, 0, [1, 2])
-        square_t(2, 0)
-        lay(4, 1, act_copy)
-        mx(0, 0, 1, [2])
+        lay(3, 0, dve_copy)
+        quant_w2(2)
+        lay(3, 1, act_copy)
+        lay_o(1, 0, act_copy)
+        lay_o(1, 1, act_copy)
+        lay_o(1, 2, dve_copy)
+        area_t(1, 0)
         lay(4, 0, dve_copy)
-        area_t(2, 0)
-        quant_w2(4)
-        mx(1, 0, 0, [0, 1])
-        quant_o(1, 1)
-        mx(0, 1, 0, [2])
-        mx(0, 1, 1, [2])
-        turn_o(2, 2)
-        turn_o(2, 1)
-        lay_o(2, 2, act_copy)
-        mx(0, 0, 1, [3])
-        mx(0, 0, 0, [3])
-        mx(0, 1, 0, [3])
-        lay_o(2, 1, act_copy)
-        mx(0, 1, 1, [3])
-        mx(1, 1, 0, [2])
-        mx(1, 0, 0, [2])
-        mx(1, 1, 0, [3])
-        turn_t(3, 1)
-        quant_o(2, 1)
-        area_t(2, 1)
+        quant_w2(3)
+        turn_t(2, 1)
         turn_o(2, 0)
-        mx(0, 0, 1, [4])
-        mx(1, 0, 0, [3])
-        mx(0, 0, 0, [4])
-        square_t(3, 1)
-        root_d2(0, 0, 1)
-        mx(0, 1, 0, [4])
-        root_d2(0, 0, 0)
-        area_t(3, 1)
-        speed_v(0, 0)
-        quant_t(2)
-        mx(0, 1, 1, [4])
-        root_d2(0, 1, 0)
-        mx(1, 1, 1, [0])
-        square_v(0, 0)
-        power_v(0, 0)
-        area_t(3, 0)
-        turn_o(3, 1)
-        mx(1, 0, 1, [0])
-        lay_o(3, 1, act_copy)
-        mx(1, 1, 0, [4])
+        turn_o(2, 1)
+        for w in range(2, 4):
+            mx_all(0, [w])
+
+        lay(4, 1, act_copy)
+        square_t(2, 0)
+        square_t(2, 1)
+        turn_t(3, 0)
+        turn_t(3, 1)
+        turn_o(2, 2)
+        area_t(1, 1)
+        nc.vector.tensor_copy(out=inflow_f[:], in_=inflow_b[:])
+        quant_o(1, 0)
+        quant_o(1, 1)
+        quant_w2(4)
         lay_o(2, 0, act_copy)
-        mx(1, 1, 1, [1, 2])
-        root_d2(0, 1, 1)
-        mx(1, 0, 0, [4])
-        root_d2(1, 0, 0)
-        square_v(0, 1)
-        mx(1, 1, 1, [3])
-        mx(2, 1, 1, [0])
-        mx(1, 0, 1, [1])
-        speed_v(0, 1)
-        quant_o(2, 0)
-        power_v(0, 1)
-        mx(1, 0, 1, [2, 3, 4])
-        mx(1, 1, 1, [4])
-        turn_o(3, 2)
-        lay_o(3, 2, dve_copy)
-        turn_o(3, 0)
-        mx(2, 0, 0, [0])
-        root_d2(1, 0, 1)
-        speed_v(1, 0)
-        root_d2(1, 1, 0)
-        root_d2(1, 1, 1)
-        speed_v(1, 1)
-        mx(2, 0, 1, [0])
-        mx(2, 0, 0, [1, 2])
-        lay_o(3, 0, act_copy)
-        mx(2, 0, 0, [3, 4])
-        mx(2, 1, 0, [0])
-        mx(2, 1, 1, [1])
-        root_d2(2, 0, 0)
-        mx(2, 0, 1, [1, 2, 3, 4])
-        quant_t(3)
-        square_v(1, 0)
-        root_d2(2, 0, 1)
-        square_v(2, 0)
-        mx(2, 1, 0, [1])
-        quant_o(3, 0)
-        power_v(1, 0)
-        speed_v(2, 0)
-        quant_o(3, 1)
-        mx(2, 1, 0, [2, 3, 4])
-        mx(3, 0, 1, [0, 1])
-        mx(3, 0, 0, [0, 1])
-        mx(2, 1, 1, [2])
-        root_d2(2, 1, 0)
-        square_v(1, 1)
-        mx(2, 1, 1, [3, 4])
-        root_d2(2, 1, 1)
-        power_v(2, 0)
-        power_v(1, 1)
-        speed_v(2, 1)
-        mx(3, 0, 1, [2])
-        mx(3, 0, 0, [2])
-        mx(3, 0, 1, [3, 4])
-        mx(3, 0, 0, [3])
-        root_d2(3, 0, 1)
-        mx(3, 0, 0, [4])
-        root_d2(3, 0, 0)
-        mx(3, 1, 1, [0, 1])
-        square_v(3, 0)
-        square_v(2, 1)
-        mx(3, 1, 0, [0, 1, 2])
-        mx(3, 1, 1, [2, 3, 4])
-        mx(3, 1, 0, [3])
-        speed_v(3, 0)
-        power_v(3, 0)
-        root_d2(3, 1, 1)
-        mx(3, 1, 0, [4])
-        square_v(3, 1, 512, 1024)
-        root_d2(3, 1, 0)
-        power_v(2, 1)
-        speed_v(3, 1, 512, 1024)
-        speed_v(3, 1, 0, 512)
-        square_v(3, 1, 0, 512)
-        power_v(3, 1, 0, 512)
-        power_v(3, 1, 512, 1024)
+        lay_o(2, 1, act_copy)
+        square_t(3, 0)
+        quant_t(1)
+        mx_all(0, [4])
+        area_t(2, 0)
+
+        groups = [(i, mt, h) for i in range(PAIRS) for mt in range(2) for h in range(2)]
+        for r in range(ROWS):
+            i, mt = divmod(r, 2)
+            last = r == ROWS - 1
+            for h in range(2):
+                root_d2(i, mt, h)
+                k = 2 * r + h + 4
+                if k < 2 * ROWS:
+                    mx(*groups[k], range(NW))
+                if last:
+                    speed_v(i, mt, h * H, (h + 1) * H)
+                    square_v(i, mt, h * H, (h + 1) * H)
+                    power_v(i, mt, h * H, (h + 1) * H)
+            if r == 0:
+                lay_o(2, 2, act_copy)
+            if r == 1:
+                square_t(3, 1)
+                lay_o(3, 0, act_copy)
+            if not last:
+                speed_v(i, mt)
+                square_v(i, mt)
+            if r == 0:
+                area_t(2, 1)
+                turn_o(3, 0)
+                turn_o(3, 1)
+                turn_o(3, 2)
+                quant_t(2)
+                quant_o(2, 0)
+                quant_o(2, 1)
+            if r == 1:
+                lay_o(3, 1, act_copy)
+                area_t(3, 0)
+                area_t(3, 1)
+            if r == 2:
+                lay_o(3, 2, act_copy)
+                quant_t(3)
+                quant_o(3, 0)
+                quant_o(3, 1)
+            if not last:
+                power_v(i, mt)

from contextlib import ExitStack

import concourse.mybir as mybir
from concourse.masks import make_identity

M, T, L, N = 1024, 1024, 1536, 1024
FLOPS = 2 * M * N * (T + L)

F32 = mybir.dt.float32
BF16 = mybir.dt.bfloat16
U32 = mybir.dt.uint32
U8 = mybir.dt.uint8
E4M3 = mybir.dt.float8_e4m3fn_x4
E5M2 = mybir.dt.float8_e5m2_x4
ACT = mybir.ActivationFunctionType
ALU = mybir.AluOpType

P = 128
KP = 512
GT = T // KP
GL = L // KP
NW = GT + GL
ROWS = M // P
PAIRS = ROWS // 2
H = 512
Q = 256


def tile_wind_farm_wakes_s2_kernel(tc, thrust, area, kern, outer, okern, inflow, speed, power):
    nc = tc.nc
    with ExitStack() as ctx:
        keep = ctx.enter_context(tc.tile_pool(name="keep", bufs=1))
        work = ctx.enter_context(tc.tile_pool(name="work", bufs=2))
        turn = ctx.enter_context(tc.psum_pool(name="turn", bufs=4))
        sums = ctx.enter_context(tc.psum_pool(name="sums", bufs=4))

        area_b = keep.tile([P, GT, 4], BF16, name="area_b")
        inflow_b = keep.tile([P, ROWS], BF16, name="inflow_b")
        nc.scalar.dma_start(out=area_b[:], in_=area.rearrange("(g p j) -> p g j", g=GT, j=4))
        nc.scalar.dma_start(out=inflow_b[:], in_=inflow.rearrange("(p t) -> p t", t=ROWS))
        ident = keep.tile([P, P], F32, name="ident")
        make_identity(nc, ident[:])
        dummy = keep.tile([P, 1], F32, name="dummy")
        nc.gpsimd.memset(dummy[:], 1.0)
        nc.scalar.activation(out=dummy[:], in_=dummy[:], func=ACT.Sqrt)
        inflow_f = keep.tile([P, ROWS], F32, name="inflow_f")

        w_hbm = [kern[g * KP:(g + 1) * KP, :] for g in range(GT)] + [okern[g * KP:(g + 1) * KP, :] for g in range(GL)]
        w_raw = {}
        t_raw = {}
        o_raw = {}

        def load_w(w, c0, width):
            raw = keep.tile([P, 4, width], BF16, name="w_raw_%d_%d" % (w, c0), align_bytes=64)
            nc.sync.dma_start(out=raw[:], in_=w_hbm[w].rearrange("(p j) n -> p j n", j=4)[:, :, c0:c0 + width])
            for c in range(c0, c0 + width, Q):
                w_raw[w, c] = raw[:, :, c - c0:]

        def load_t(i):
            t_raw[i] = work.tile([P, 2, T], BF16, name="t_raw", bufs=3, align_bytes=64)
            nc.sync.dma_start(out=t_raw[i][:], in_=thrust.rearrange("(p t) k -> p t k", t=ROWS)[:, 2 * i:2 * i + 2, :])

        def load_o(i):
            o_raw[i] = work.tile([P, 2, L], BF16, name="o_raw", bufs=3, align_bytes=64)
            nc.sync.dma_start(out=o_raw[i][:], in_=outer.rearrange("(p t) k -> p t k", t=ROWS)[:, 2 * i:2 * i + 2, :])

        w_codes = [keep.tile([P, N], U32, name="w_codes_%d" % w, align_bytes=64) for w in range(NW)]
        w_scales = [keep.tile([P, N], U8, name="w_scales_%d" % w, align_bytes=64) for w in range(NW)]
        w_lay = {}

        def lay(w, h, copy, c0=0, c1=H):
            if (w, 0) not in w_lay:
                w_lay[w, 0] = work.tile([P, N, 4], BF16, name="w_lay", bufs=3, align_bytes=64)
            copy(
                out=w_lay[w, 0][:, h * H + c0:h * H + c1].rearrange("p (c i) j -> p c j i", i=4),
                in_=w_raw[w, h * H + c0][:, :, 0:c1 - c0].rearrange("p j (c i) -> p c j i", i=4),
            )

        def quant_w(w, h):
            cols = slice(h * H, (h + 1) * H)
            nc.vector.quantize_mx(
                out=w_codes[w][:, cols].bitcast(E4M3),
                scales=w_scales[w][:, cols],
                in_=w_lay[w, 0][:, cols].rearrange("p c j -> p (c j)"),
            )

        x_codes = {}
        x_scales = {}
        for i in range(PAIRS):
            x_codes[i] = keep.tile([P, NW, 2 * P], U32, name="x_codes_%d" % i, align_bytes=64)
            x_scales[i] = keep.tile([P, NW, 2 * P], U8, name="x_scales_%d" % i, align_bytes=64)

        banks = {}

        def turn_x(raw, g):
            bank = turn.tile([P, 2, 2 * P], F32, name="bank")
            words = raw[:].bitcast(F32)
            for mt in range(2):
                for u in range(2):
                    nc.tensor.transpose(
                        bank[:, u, mt * P:(mt + 1) * P],
                        words[:, mt, 256 * g + u:256 * (g + 1):2],
                        ident[:],
                    )
            return bank

        def turn_t(i, g):
            banks["t", i, g] = turn_x(t_raw[i], g)

        def turn_o(i, g):
            banks["o", i, g] = turn_x(o_raw[i], g)

        t_sq = {}
        t_a = {}
        o_lay = {}


        def square_t(i, g):
            if i not in t_sq:
                t_sq[i] = work.tile([P, GT, 2 * P, 4], F32, name="t_sq", bufs=2, align_bytes=64)
            nc.scalar.activation(
                out=t_sq[i][:, g].rearrange("p c (u e) -> p c u e", e=2),
                in_=banks["t", i, g][:].bitcast(BF16).rearrange("p u (c e) -> p c u e", e=2),
                func=ACT.Square,
            )

        def area_t(i, g):
            if i not in t_a:
                t_a[i] = work.tile([P, GT, 2 * P, 4], BF16, name="t_a", bufs=2, align_bytes=64)
            nc.vector.tensor_tensor(
                out=t_a[i][:, g],
                in0=t_sq[i][:, g],
                in1=area_b[:, g, :].unsqueeze(1).to_broadcast([P, 2 * P, 4]),
                op=ALU.mult,
            )

        def quant_w2(w):
            nc.vector.quantize_mx(
                out=w_codes[w][:].bitcast(E4M3),
                scales=w_scales[w][:],
                in_=w_lay[w, 0][:].rearrange("p c j -> p (c j)"),
            )

        def quant_t(i):
            nc.vector.quantize_mx(
                out=x_codes[i][:, 0:GT, :].rearrange("p g c -> p (g c)").bitcast(E5M2),
                scales=x_scales[i][:, 0:GT, :].rearrange("p g c -> p (g c)"),
                in_=t_a[i][:].rearrange("p g c j -> p (g c j)"),
            )

        def lay_o(i, g, copy):
            if i not in o_lay:
                o_lay[i] = work.tile([P, GL, 2 * P, 2], F32, name="o_lay", bufs=2, align_bytes=64)
            copy(out=o_lay[i][:, g], in_=banks["o", i, g][:].rearrange("p u c -> p c u"))

        def quant_o(i, part):
            src = o_lay[i][:].rearrange("p g c u -> p g (c u)").bitcast(BF16)
            for g0, g1 in (((0, 2), (2, 3))[part],):
                nc.vector.quantize_mx(
                    out=x_codes[i][:, GT + g0:GT + g1, :].rearrange("p g c -> p (g c)").bitcast(E4M3),
                    scales=x_scales[i][:, GT + g0:GT + g1, :].rearrange("p g c -> p (g c)"),
                    in_=src[:, g0:g1, :].rearrange("p g c -> p (g c)"),
                )

        acc = {}

        def mx(i, mt, h, passes):
            if (i, mt, h) not in acc:
                acc[i, mt, h] = sums.tile([P, H], F32, name="acc")
            rows = slice(mt * P, (mt + 1) * P)
            cols = slice(h * H, (h + 1) * H)
            for w in passes:
                nc.tensor.matmul_mx(
                    out=acc[i, mt, h][:],
                    lhsT=x_codes[i][:, w, rows].bitcast(E5M2 if w < GT else E4M3),
                    lhsT_scale=x_scales[i][:, w, rows],
                    rhs=w_codes[w][:, cols].bitcast(E4M3),
                    rhs_scale=w_scales[w][:, cols],
                    start=(w == 0),
                    stop=(w == NW - 1),
                )

        def mx_all(i, passes):
            for mt in range(2):
                for h in range(2):
                    mx(i, mt, h, passes)

        root = {}
        vel = {}
        vel2 = {}
        pw = {}

        def root_d2(i, mt, h):
            if (i, mt) not in root:
                root[i, mt] = work.tile([P, N], F32, name="root", bufs=3)
            nc.scalar.activation(out=root[i, mt][:, h * H:(h + 1) * H], in_=acc[i, mt, h][:], func=ACT.Sqrt)

        def square_v(i, mt, c0=0, c1=N):
            r = 2 * i + mt
            if (i, mt) not in vel2:
                vel2[i, mt] = work.tile([P, N], F32, name="vel2", bufs=2)
            nc.scalar.activation(
                out=vel2[i, mt][:, c0:c1], in_=root[i, mt][:, c0:c1], func=ACT.Square, scale=-1.0, bias=inflow_f[:, r:r + 1]
            )

        def speed_v(i, mt, c0=0, c1=N):
            r = 2 * i + mt
            if (i, mt) not in vel:
                vel[i, mt] = work.tile([P, N], F32, name="vel", bufs=4)
            nc.vector.tensor_scalar(
                out=vel[i, mt][:, c0:c1], in0=root[i, mt][:, c0:c1], scalar1=-1.0, scalar2=inflow_f[:, r:r + 1],
                op0=ALU.mult, op1=ALU.add,
            )
            nc.sync.dma_start(out=speed.rearrange("(p t) n -> p t n", t=ROWS)[:, r, c0:c1], in_=vel[i, mt][:, c0:c1])

        def square_dve(i, mt, c0, c1):
            nc.vector.tensor_tensor(
                out=vel2[i, mt][:, c0:c1], in0=vel[i, mt][:, c0:c1], in1=vel[i, mt][:, c0:c1], op=ALU.mult
            )

        def power_v(i, mt, c0=0, c1=N):
            r = 2 * i + mt
            if (i, mt) not in pw:
                pw[i, mt] = work.tile([P, N], F32, name="pw", bufs=4)
            nc.vector.tensor_tensor(
                out=pw[i, mt][:, c0:c1], in0=vel2[i, mt][:, c0:c1], in1=vel[i, mt][:, c0:c1], op=ALU.mult
            )
            nc.sync.dma_start(out=power.rearrange("(p t) n -> p t n", t=ROWS)[:, r, c0:c1], in_=pw[i, mt][:, c0:c1])

        act_copy = nc.scalar.copy
        dve_copy = nc.vector.tensor_copy

        load_w(0, 0, H)
        load_t(0)
        load_w(0, H, H)
        load_o(0)
        load_w(1, 0, N)
        load_t(1)
        load_w(2, 0, N)
        load_w(3, 0, N)
        load_o(1)
        load_w(4, 0, N)
        load_t(2)
        load_o(2)

        lay(0, 0, act_copy, 0, Q)
        lay(0, 0, dve_copy, Q, H)
        turn_t(0, 0)
        turn_t(0, 1)
        square_t(0, 0)
        square_t(0, 1)
        quant_w(0, 0)
        lay(0, 1, dve_copy)
        turn_o(0, 0)
        turn_o(0, 1)
        turn_o(0, 2)
        lay_o(0, 0, act_copy)
        lay_o(0, 1, act_copy)
        area_t(0, 0)
        area_t(0, 1)
        lay_o(0, 2, act_copy)
        quant_w(0, 1)
        lay(1, 1, act_copy)
        lay(1, 0, dve_copy)
        turn_t(1, 0)
        turn_t(1, 1)
        square_t(1, 0)
        quant_t(0)
        quant_o(0, 0)
        quant_o(0, 1)
        quant_w2(1)
        for w in range(2):
            mx_all(0, [w])

        lay(2, 0, dve_copy)
        lay(2, 1, act_copy)
        square_t(1, 1)
        turn_o(1, 0)
        turn_o(1, 1)
        turn_o(1, 2)
        load_t(3)
        load_o(3)
        turn_t(2, 0)
        lay(3, 0, dve_copy)
        quant_w2(2)
        lay(3, 1, act_copy)
        lay_o(1, 0, act_copy)
        lay_o(1, 1, act_copy)
        lay_o(1, 2, dve_copy)
        area_t(1, 0)
        lay(4, 0, dve_copy)
        quant_w2(3)
        turn_t(2, 1)
        turn_o(2, 0)
        turn_o(2, 1)
        for w in range(2, 4):
            mx_all(0, [w])

        lay(4, 1, act_copy)
        square_t(2, 0)
        square_t(2, 1)
        turn_t(3, 0)
        turn_t(3, 1)
        turn_o(2, 2)
        area_t(1, 1)
        nc.vector.tensor_copy(out=inflow_f[:], in_=inflow_b[:])
        quant_o(1, 0)
        quant_o(1, 1)
        quant_w2(4)
        lay_o(2, 0, act_copy)
        lay_o(2, 1, act_copy)
        square_t(3, 0)
        quant_t(1)
        mx_all(0, [4])
        area_t(2, 0)

        groups = [(i, mt, h) for i in range(PAIRS) for mt in range(2) for h in range(2)]
        for r in range(ROWS):
            i, mt = divmod(r, 2)
            last = r == ROWS - 1
            for h in range(2):
                root_d2(i, mt, h)
                k = 2 * r + h + 4
                if k < 2 * ROWS:
                    mx(*groups[k], range(NW))
                if last:
                    speed_v(i, mt, h * H, (h + 1) * H)
                    square_v(i, mt, h * H, (h + 1) * H)
                    power_v(i, mt, h * H, (h + 1) * H)
            if r == 0:
                lay_o(2, 2, act_copy)
            if r == 1:
                square_t(3, 1)
                lay_o(3, 0, act_copy)
            if not last:
                speed_v(i, mt)
                square_v(i, mt)
            if r == 0:
                area_t(2, 1)
                turn_o(3, 0)
                turn_o(3, 1)
                turn_o(3, 2)
                quant_t(2)
                quant_o(2, 0)
                quant_o(2, 1)
            if r == 1:
                lay_o(3, 1, act_copy)
                area_t(3, 0)
                area_t(3, 1)
            if r == 2:
                lay_o(3, 2, act_copy)
                quant_t(3)
                quant_o(3, 0)
                quant_o(3, 1)
            if not last:
                power_v(i, mt)
